import numpy as np
import ml_dtypes

BF16 = ml_dtypes.bfloat16


def bf(x):
    return np.asarray(x, np.float32).astype(BF16)


def f32(x):
    return np.asarray(x, np.float32)


def f64(x):
    return np.asarray(x).astype(np.float64)


def striped(idx):
    return np.tile(idx.reshape(-1, 16).T, (8, 1))


def rows(idx, k):
    return np.tile(idx, (k, 1))


def look(tab, idx):
    return np.take_along_axis(f64(tab), rows(idx, len(tab)), axis=1)


K, S, D, V, N = 256, 2048, 2, 512, 1024


def setup_inputs():
    return {"tab": f32(np.random.standard_normal((2, K, S))), "t": f32(0.5 * np.random.standard_normal((K, V))), "offs": striped(np.random.permutation(S)[:N])}


def reference(tab, t, offs):
    idx = offs[:16].T.reshape(-1)
    a = [look(tab[1], idx[d * V:(d + 1) * V]) + f64(t) for d in range(D)]
    e = [np.exp(np.maximum(v, 0.2 * v)) for v in a]
    x = sum(e[d] * look(tab[0], idx[d * V:(d + 1) * V]) for d in range(D)) / sum(e)
    return x

@@ -1,0 +1,75 @@
+import concourse.mybir as mybir
+
+F32, U16 = mybir.dt.float32, mybir.dt.uint16
+ADD, SUB = mybir.AluOpType.add, mybir.AluOpType.subtract
+MULT, MAX = mybir.AluOpType.mult, mybir.AluOpType.max
+EXP = mybir.ActivationFunctionType.Exp
+
+P = 128
+ROWS = 256
+NODES = 2048
+TARGETS = 512
+NEIGHBOURS = 2
+BLOCKS = ROWS // P
+LIST_COLUMNS = TARGETS // 16
+SLOPE = 0.2
+
+
+def tile_lookup_gat_out_kernel(tc, tab, t, offs, out):
+    nc = tc.nc
+    with (
+        tc.tile_pool(name="held", bufs=1) as held,
+        tc.tile_pool(name="work", bufs=BLOCKS) as work,
+    ):
+        offsets = held.tile([P, NEIGHBOURS * LIST_COLUMNS], U16, name="offsets")
+        nc.sync.dma_start(offsets[:], offs)
+        own = [held.tile([P, TARGETS], F32, name=f"own{b}") for b in range(BLOCKS)]
+        scores = [held.tile([P, NODES], F32, name=f"scores{b}") for b in range(BLOCKS)]
+        values = [held.tile([P, NODES], F32, name=f"values{b}") for b in range(BLOCKS)]
+        for b in range(BLOCKS):
+            rows = slice(b * P, (b + 1) * P)
+            nc.sync.dma_start(own[b][:], t[rows, :])
+            nc.sync.dma_start(scores[b][:], tab[1, rows, :])
+        for b in range(BLOCKS):
+            rows = slice(b * P, (b + 1) * P)
+            nc.sync.dma_start(values[b][:], tab[0, rows, :])
+
+        def entries(d):
+            return offsets[:, d * LIST_COLUMNS:(d + 1) * LIST_COLUMNS]
+
+        weights = []
+        for b in range(BLOCKS):
+            leaky = []
+            for d in range(NEIGHBOURS):
+                a = work.tile([P, TARGETS], F32, name=f"a{d}")
+                nc.vector.tensor_tensor(a[:], scores[b][:].indirect(entries(d)), own[b][:], ADD)
+                l = work.tile([P, TARGETS], F32, name=f"l{d}")
+                nc.vector.scalar_tensor_tensor(l[:], a[:], SLOPE, a[:], MULT, MAX)
+                leaky.append(l)
+            top = work.tile([P, TARGETS], F32, name="top")
+            nc.vector.tensor_tensor(top[:], leaky[0][:], leaky[1][:], MAX)
+            e = []
+            for d in range(NEIGHBOURS):
+                below = work.tile([P, TARGETS], F32, name=f"below{d}")
+                nc.vector.tensor_tensor(below[:], leaky[d][:], top[:], SUB)
+                e_d = work.tile([P, TARGETS], F32, name=f"e{d}")
+                nc.scalar.activation(e_d[:], below[:], EXP)
+                e.append(e_d)
+            weights.append(e)
+
+        for b in range(BLOCKS):
+            e = weights[b]
+            total = work.tile([P, TARGETS], F32, name="total")
+            nc.vector.tensor_tensor(total[:], e[0][:], e[1][:], ADD)
+            inverse = work.tile([P, TARGETS], F32, name="inverse")
+            nc.vector.reciprocal(inverse[:], total[:])
+            products = []
+            for d in range(NEIGHBOURS):
+                product = work.tile([P, TARGETS], F32, name=f"product{d}")
+                nc.vector.tensor_tensor(product[:], values[b][:].indirect(entries(d)), e[d][:], MULT)
+                products.append(product)
+            numerator = work.tile([P, TARGETS], F32, name="numerator")
+            nc.vector.tensor_tensor(numerator[:], products[0][:], products[1][:], ADD)
+            x = work.tile([P, TARGETS], F32, name="x")
+            nc.vector.tensor_tensor(x[:], numerator[:], inverse[:], MULT)
+            nc.sync.dma_start(out[b * P:(b + 1) * P, :], x[:])

@@ -3,7 +3,7 @@ import concourse.mybir as mybir
 F32, U16 = mybir.dt.float32, mybir.dt.uint16
 ADD, SUB = mybir.AluOpType.add, mybir.AluOpType.subtract
 MULT, MAX = mybir.AluOpType.mult, mybir.AluOpType.max
-EXP = mybir.ActivationFunctionType.Exp
+SIGMOID = mybir.ActivationFunctionType.Sigmoid
 
 P = 128
 ROWS = 256
@@ -46,30 +46,21 @@ def tile_lookup_gat_out_kernel(tc, tab, t, offs, out):
                 l = work.tile([P, TARGETS], F32, name=f"l{d}")
                 nc.vector.scalar_tensor_tensor(l[:], a[:], SLOPE, a[:], MULT, MAX)
                 leaky.append(l)
-            top = work.tile([P, TARGETS], F32, name="top")
-            nc.vector.tensor_tensor(top[:], leaky[0][:], leaky[1][:], MAX)
-            e = []
-            for d in range(NEIGHBOURS):
-                below = work.tile([P, TARGETS], F32, name=f"below{d}")
-                nc.vector.tensor_tensor(below[:], leaky[d][:], top[:], SUB)
-                e_d = work.tile([P, TARGETS], F32, name=f"e{d}")
-                nc.scalar.activation(e_d[:], below[:], EXP)
-                e.append(e_d)
-            weights.append(e)
+            lead = work.tile([P, TARGETS], F32, name="lead")
+            nc.vector.tensor_tensor(lead[:], leaky[0][:], leaky[1][:], SUB)
+            share = []
+            for d, sign in enumerate((1.0, -1.0)):
+                s = work.tile([P, TARGETS], F32, name=f"share{d}")
+                nc.scalar.activation(s[:], lead[:], SIGMOID, scale=sign)
+                share.append(s)
+            weights.append(share)
 
         for b in range(BLOCKS):
-            e = weights[b]
-            total = work.tile([P, TARGETS], F32, name="total")
-            nc.vector.tensor_tensor(total[:], e[0][:], e[1][:], ADD)
-            inverse = work.tile([P, TARGETS], F32, name="inverse")
-            nc.vector.reciprocal(inverse[:], total[:])
             products = []
             for d in range(NEIGHBOURS):
                 product = work.tile([P, TARGETS], F32, name=f"product{d}")
-                nc.vector.tensor_tensor(product[:], values[b][:].indirect(entries(d)), e[d][:], MULT)
+                nc.vector.tensor_tensor(product[:], values[b][:].indirect(entries(d)), weights[b][d][:], MULT)
                 products.append(product)
-            numerator = work.tile([P, TARGETS], F32, name="numerator")
-            nc.vector.tensor_tensor(numerator[:], products[0][:], products[1][:], ADD)
             x = work.tile([P, TARGETS], F32, name="x")
-            nc.vector.tensor_tensor(x[:], numerator[:], inverse[:], MULT)
+            nc.vector.tensor_tensor(x[:], products[0][:], products[1][:], ADD)
             nc.sync.dma_start(out[b * P:(b + 1) * P, :], x[:])

@@ -1,9 +1,10 @@
+import concourse.masks as masks
 import concourse.mybir as mybir
 
 F32, U16 = mybir.dt.float32, mybir.dt.uint16
 ADD, SUB = mybir.AluOpType.add, mybir.AluOpType.subtract
 MULT, MAX = mybir.AluOpType.mult, mybir.AluOpType.max
-SIGMOID = mybir.ActivationFunctionType.Sigmoid
+RELU, SIGMOID = mybir.ActivationFunctionType.Relu, mybir.ActivationFunctionType.Sigmoid
 
 P = 128
 ROWS = 256
@@ -19,48 +20,83 @@ def tile_lookup_gat_out_kernel(tc, tab, t, offs, out):
     nc = tc.nc
     with (
         tc.tile_pool(name="held", bufs=1) as held,
-        tc.tile_pool(name="work", bufs=BLOCKS) as work,
+        tc.psum_pool(name="sums", bufs=1) as sums,
     ):
         offsets = held.tile([P, NEIGHBOURS * LIST_COLUMNS], U16, name="offsets")
         nc.sync.dma_start(offsets[:], offs)
         own = [held.tile([P, TARGETS], F32, name=f"own{b}") for b in range(BLOCKS)]
         scores = [held.tile([P, NODES], F32, name=f"scores{b}") for b in range(BLOCKS)]
         values = [held.tile([P, NODES], F32, name=f"values{b}") for b in range(BLOCKS)]
-        for b in range(BLOCKS):
+        for b in (0, 1):
             rows = slice(b * P, (b + 1) * P)
             nc.sync.dma_start(own[b][:], t[rows, :])
             nc.sync.dma_start(scores[b][:], tab[1, rows, :])
-        for b in range(BLOCKS):
-            rows = slice(b * P, (b + 1) * P)
-            nc.sync.dma_start(values[b][:], tab[0, rows, :])
+        for b in (1, 0):
+            nc.sync.dma_start(values[b][:], tab[0, b * P:(b + 1) * P, :])
+
+        plus = held.tile([P, P], F32, name="plus")
+        masks.make_identity(nc, plus[:])
+        minus = held.tile([P, P], F32, name="minus")
+        nc.gpsimd.tensor_scalar(minus[:], plus[:], -1.0, None, MULT)
+
+        first = held.tile([P, 1], F32, name="first")
+        nc.gpsimd.memset(first[:], 0.0)
+        half = held.tile([P, 1], F32, name="half")
+        nc.scalar.activation(half[:], first[:], SIGMOID)
 
         def entries(d):
             return offsets[:, d * LIST_COLUMNS:(d + 1) * LIST_COLUMNS]
 
-        weights = []
-        for b in range(BLOCKS):
-            leaky = []
-            for d in range(NEIGHBOURS):
-                a = work.tile([P, TARGETS], F32, name=f"a{d}")
-                nc.vector.tensor_tensor(a[:], scores[b][:].indirect(entries(d)), own[b][:], ADD)
-                l = work.tile([P, TARGETS], F32, name=f"l{d}")
-                nc.vector.scalar_tensor_tensor(l[:], a[:], SLOPE, a[:], MULT, MAX)
-                leaky.append(l)
-            lead = work.tile([P, TARGETS], F32, name="lead")
-            nc.vector.tensor_tensor(lead[:], leaky[0][:], leaky[1][:], SUB)
-            share = []
-            for d, sign in enumerate((1.0, -1.0)):
-                s = work.tile([P, TARGETS], F32, name=f"share{d}")
-                nc.scalar.activation(s[:], lead[:], SIGMOID, scale=sign)
-                share.append(s)
-            weights.append(share)
+        def look_up_score(b, d):
+            a = held.tile([P, TARGETS], F32, name=f"a{b}{d}")
+            nc.vector.tensor_tensor(a[:], scores[b][:].indirect(entries(d)), own[b][:], ADD)
+            return a
 
-        for b in range(BLOCKS):
-            products = []
+        def shares(b, lead, scale):
+            result = []
+            for d, sign in enumerate((1.0, -1.0)):
+                share = held.tile([P, TARGETS], F32, name=f"share{b}{d}")
+                nc.scalar.activation(share[:], lead[:], SIGMOID, scale=sign * scale)
+                result.append(share)
+            return result
+
+        def look_up_values(b, share):
+            result = []
             for d in range(NEIGHBOURS):
-                product = work.tile([P, TARGETS], F32, name=f"product{d}")
-                nc.vector.tensor_tensor(product[:], values[b][:].indirect(entries(d)), weights[b][d][:], MULT)
-                products.append(product)
-            x = work.tile([P, TARGETS], F32, name="x")
-            nc.vector.tensor_tensor(x[:], products[0][:], products[1][:], ADD)
-            nc.sync.dma_start(out[b * P:(b + 1) * P, :], x[:])
+                product = held.tile([P, TARGETS], F32, name=f"product{b}{d}")
+                nc.vector.tensor_tensor(product[:], values[b][:].indirect(entries(d)), share[d][:], MULT)
+                result.append(product)
+            return result
+
+        lead0 = sums.tile([P, TARGETS], F32, name="lead0")
+        for d, weights in enumerate((plus, minus)):
+            a = look_up_score(0, d)
+            bend = held.tile([P, TARGETS], F32, name=f"bend{d}")
+            nc.scalar.activation(bend[:], a[:], RELU, scale=1.0 / SLOPE - 1.0)
+            nc.tensor.matmul(lead0[:], weights[:], a[:], start=d == 0, stop=False)
+            nc.tensor.matmul(lead0[:], weights[:], bend[:], start=False, stop=d == 1)
+
+        leaky = []
+        for d in range(NEIGHBOURS):
+            a = look_up_score(1, d)
+            l = held.tile([P, TARGETS], F32, name=f"l{d}")
+            nc.vector.scalar_tensor_tensor(l[:], a[:], SLOPE, a[:], MULT, MAX)
+            leaky.append(l)
+        lead1 = held.tile([P, TARGETS], F32, name="lead1")
+        nc.vector.tensor_tensor(lead1[:], leaky[0][:], leaky[1][:], SUB)
+
+        share1 = shares(1, lead1, 1.0)
+        share0 = shares(0, lead0, SLOPE)
+
+        product1 = look_up_values(1, share1)
+        total1 = sums.tile([P, TARGETS], F32, name="total1")
+        for d in range(NEIGHBOURS):
+            nc.tensor.matmul(total1[:], plus[:], product1[d][:], start=d == 0, stop=d == 1)
+        x1 = held.tile([P, TARGETS], F32, name="x1")
+        nc.scalar.copy(x1[:], total1[:])
+        nc.sync.dma_start(out[P:2 * P, :], x1[:])
+
+        product0 = look_up_values(0, share0)
+        x0 = held.tile([P, TARGETS], F32, name="x0")
+        nc.vector.tensor_tensor(x0[:], product0[0][:], product0[1][:], ADD)
+        nc.sync.dma_start(out[0:P, :], x0[:])

@@ -14,6 +14,7 @@ NEIGHBOURS = 2
 BLOCKS = ROWS // P
 LIST_COLUMNS = TARGETS // 16
 SLOPE = 0.2
+HALF = TARGETS // 2
 
 
 def tile_lookup_gat_out_kernel(tc, tab, t, offs, out):
@@ -31,7 +32,7 @@ def tile_lookup_gat_out_kernel(tc, tab, t, offs, out):
             rows = slice(b * P, (b + 1) * P)
             nc.sync.dma_start(own[b][:], t[rows, :])
             nc.sync.dma_start(scores[b][:], tab[1, rows, :])
-        for b in (1, 0):
+        for b in range(BLOCKS):
             nc.sync.dma_start(values[b][:], tab[0, b * P:(b + 1) * P, :])
 
         plus = held.tile([P, P], F32, name="plus")
@@ -39,64 +40,74 @@ def tile_lookup_gat_out_kernel(tc, tab, t, offs, out):
         minus = held.tile([P, P], F32, name="minus")
         nc.gpsimd.tensor_scalar(minus[:], plus[:], -1.0, None, MULT)
 
-        first = held.tile([P, 1], F32, name="first")
-        nc.gpsimd.memset(first[:], 0.0)
-        half = held.tile([P, 1], F32, name="half")
-        nc.scalar.activation(half[:], first[:], SIGMOID)
+        nothing = held.tile([P, 1], F32, name="nothing")
+        nc.gpsimd.memset(nothing[:], 0.0)
+        warmed = held.tile([P, 1], F32, name="warmed")
+        nc.scalar.activation(warmed[:], nothing[:], SIGMOID)
 
-        def entries(d):
-            return offsets[:, d * LIST_COLUMNS:(d + 1) * LIST_COLUMNS]
+        def entries(d, first, count):
+            start = (d * TARGETS + first) // 16
+            return offsets[:, start:start + count // 16]
 
-        def look_up_score(b, d):
-            a = held.tile([P, TARGETS], F32, name=f"a{b}{d}")
-            nc.vector.tensor_tensor(a[:], scores[b][:].indirect(entries(d)), own[b][:], ADD)
-            return a
+        def tiles(kind):
+            return [[held.tile([P, TARGETS], F32, name=f"{kind}{b}{d}") for d in range(NEIGHBOURS)] for b in range(BLOCKS)]
 
-        def shares(b, lead, scale):
-            result = []
-            for d, sign in enumerate((1.0, -1.0)):
-                share = held.tile([P, TARGETS], F32, name=f"share{b}{d}")
-                nc.scalar.activation(share[:], lead[:], SIGMOID, scale=sign * scale)
-                result.append(share)
-            return result
+        a, bent, share, product = tiles("a"), tiles("bent"), tiles("share"), tiles("product")
+        x = [held.tile([P, TARGETS], F32, name=f"x{b}") for b in range(BLOCKS)]
+        halves = [slice(h * HALF, (h + 1) * HALF) for h in range(2)]
 
-        def look_up_values(b, share):
-            result = []
+        def look_up_scores(b):
             for d in range(NEIGHBOURS):
-                product = held.tile([P, TARGETS], F32, name=f"product{b}{d}")
-                nc.vector.tensor_tensor(product[:], values[b][:].indirect(entries(d)), share[d][:], MULT)
-                result.append(product)
-            return result
+                nc.vector.tensor_tensor(a[b][d][:], scores[b][:].indirect(entries(d, 0, TARGETS)), own[b][:], ADD)
 
-        lead0 = sums.tile([P, TARGETS], F32, name="lead0")
-        for d, weights in enumerate((plus, minus)):
-            a = look_up_score(0, d)
-            bend = held.tile([P, TARGETS], F32, name=f"bend{d}")
-            nc.scalar.activation(bend[:], a[:], RELU, scale=1.0 / SLOPE - 1.0)
-            nc.tensor.matmul(lead0[:], weights[:], a[:], start=d == 0, stop=False)
-            nc.tensor.matmul(lead0[:], weights[:], bend[:], start=False, stop=d == 1)
+        def make_shares(b, half, lead, scale):
+            for d, sign in enumerate((1.0, -1.0)):
+                nc.scalar.activation(share[b][d][:, half], lead, SIGMOID, scale=sign * scale)
 
-        leaky = []
-        for d in range(NEIGHBOURS):
-            a = look_up_score(1, d)
-            l = held.tile([P, TARGETS], F32, name=f"l{d}")
-            nc.vector.scalar_tensor_tensor(l[:], a[:], SLOPE, a[:], MULT, MAX)
-            leaky.append(l)
-        lead1 = held.tile([P, TARGETS], F32, name="lead1")
-        nc.vector.tensor_tensor(lead1[:], leaky[0][:], leaky[1][:], SUB)
+        def weigh_on_tensor(b, h):
+            half = halves[h]
+            lead = sums.tile([P, HALF], F32, name=f"lead{b}{h}")
+            for d, weights in enumerate((plus, minus)):
+                nc.scalar.activation(bent[b][d][:, half], a[b][d][:, half], RELU, scale=1.0 / SLOPE - 1.0)
+                nc.tensor.matmul(lead[:, 0:HALF], weights[:], a[b][d][:, half], start=d == 0, stop=False)
+                nc.tensor.matmul(lead[:, 0:HALF], weights[:], bent[b][d][:, half], start=False, stop=d == 1)
+            make_shares(b, half, lead[:, 0:HALF], SLOPE)
 
-        share1 = shares(1, lead1, 1.0)
-        share0 = shares(0, lead0, SLOPE)
+        def weigh_on_vector(b, h):
+            half = halves[h]
+            for d in range(NEIGHBOURS):
+                nc.vector.scalar_tensor_tensor(bent[b][d][:, half], a[b][d][:, half], SLOPE, a[b][d][:, half], MULT, MAX)
+            lead = held.tile([P, HALF], F32, name=f"lead{b}{h}")
+            nc.vector.tensor_tensor(lead[:], bent[b][0][:, half], bent[b][1][:, half], SUB)
+            make_shares(b, half, lead[:], 1.0)
 
-        product1 = look_up_values(1, share1)
-        total1 = sums.tile([P, TARGETS], F32, name="total1")
-        for d in range(NEIGHBOURS):
-            nc.tensor.matmul(total1[:], plus[:], product1[d][:], start=d == 0, stop=d == 1)
-        x1 = held.tile([P, TARGETS], F32, name="x1")
-        nc.scalar.copy(x1[:], total1[:])
-        nc.sync.dma_start(out[P:2 * P, :], x1[:])
+        def look_up_values(b, h):
+            half = halves[h]
+            for d in range(NEIGHBOURS):
+                picked = values[b][:].indirect(entries(d, h * HALF, HALF))
+                nc.vector.tensor_tensor(product[b][d][:, half], picked, share[b][d][:, half], MULT)
 
-        product0 = look_up_values(0, share0)
-        x0 = held.tile([P, TARGETS], F32, name="x0")
-        nc.vector.tensor_tensor(x0[:], product0[0][:], product0[1][:], ADD)
-        nc.sync.dma_start(out[0:P, :], x0[:])
+        def add_on_tensor(b, h):
+            half = halves[h]
+            total = sums.tile([P, HALF], F32, name=f"total{b}{h}")
+            for d in range(NEIGHBOURS):
+                nc.tensor.matmul(total[:, 0:HALF], plus[:], product[b][d][:, half], start=d == 0, stop=d == 1)
+            nc.scalar.copy(x[b][:, half], total[:, 0:HALF])
+
+        def add_on_vector(b, h):
+            half = halves[h]
+            nc.vector.tensor_tensor(x[b][:, half], product[b][0][:, half], product[b][1][:, half], ADD)
+
+        def store(b, h):
+            nc.sync.dma_start(out[b * P:(b + 1) * P, halves[h]], x[b][:, halves[h]])
+
+        look_up_scores(0)
+        weigh_on_tensor(0, 0)
+        weigh_on_tensor(0, 1)
+        look_up_scores(1)
+        weigh_on_vector(1, 0)
+        weigh_on_tensor(1, 1)
+        for b, h, add in ((0, 0, add_on_tensor), (1, 0, add_on_tensor), (0, 1, add_on_vector), (1, 1, add_on_vector)):
+            look_up_values(b, h)
+            add(b, h)
+            store(b, h)

@@ -1,7 +1,7 @@
 import concourse.masks as masks
 import concourse.mybir as mybir
 
-F32, U16 = mybir.dt.float32, mybir.dt.uint16
+F32, BF16, U16 = mybir.dt.float32, mybir.dt.bfloat16, mybir.dt.uint16
 ADD, SUB = mybir.AluOpType.add, mybir.AluOpType.subtract
 MULT, MAX = mybir.AluOpType.mult, mybir.AluOpType.max
 RELU, SIGMOID = mybir.ActivationFunctionType.Relu, mybir.ActivationFunctionType.Sigmoid
@@ -15,6 +15,7 @@ BLOCKS = ROWS // P
 LIST_COLUMNS = TARGETS // 16
 SLOPE = 0.2
 HALF = TARGETS // 2
+WARM_UPS = 16
 
 
 def tile_lookup_gat_out_kernel(tc, tab, t, offs, out):
@@ -34,6 +35,12 @@ def tile_lookup_gat_out_kernel(tc, tab, t, offs, out):
             nc.sync.dma_start(scores[b][:], tab[1, rows, :])
         for b in range(BLOCKS):
             nc.sync.dma_start(values[b][:], tab[0, b * P:(b + 1) * P, :])
+
+        zeros = held.tile([P, TARGETS], BF16, name="zeros")
+        nc.vector.memset(zeros[:], 0.0)
+        unread = sums.tile([P, TARGETS], F32, name="unread")
+        for i in range(WARM_UPS):
+            nc.tensor.matmul(unread[:], zeros[:, 0:P], zeros[:], start=True, stop=True)
 
         plus = held.tile([P, P], F32, name="plus")
         masks.make_identity(nc, plus[:])
@@ -107,7 +114,10 @@ def tile_lookup_gat_out_kernel(tc, tab, t, offs, out):
         look_up_scores(1)
         weigh_on_vector(1, 0)
         weigh_on_tensor(1, 1)
-        for b, h, add in ((0, 0, add_on_tensor), (1, 0, add_on_tensor), (0, 1, add_on_vector), (1, 1, add_on_vector)):
+        for b, h in ((0, 0), (1, 0), (0, 1)):
             look_up_values(b, h)
-            add(b, h)
+            add_on_tensor(b, h)
             store(b, h)
+        look_up_values(1, 1)
+        add_on_vector(1, 1)
+        store(1, 1)

import concourse.masks as masks
import concourse.mybir as mybir

F32, BF16, U16 = mybir.dt.float32, mybir.dt.bfloat16, mybir.dt.uint16
ADD, SUB = mybir.AluOpType.add, mybir.AluOpType.subtract
MULT, MAX = mybir.AluOpType.mult, mybir.AluOpType.max
RELU, SIGMOID = mybir.ActivationFunctionType.Relu, mybir.ActivationFunctionType.Sigmoid

P = 128
ROWS = 256
NODES = 2048
TARGETS = 512
NEIGHBOURS = 2
BLOCKS = ROWS // P
LIST_COLUMNS = TARGETS // 16
SLOPE = 0.2
HALF = TARGETS // 2
WARM_UPS = 16


def tile_lookup_gat_out_kernel(tc, tab, t, offs, out):
    nc = tc.nc
    with (
        tc.tile_pool(name="held", bufs=1) as held,
        tc.psum_pool(name="sums", bufs=1) as sums,
    ):
        offsets = held.tile([P, NEIGHBOURS * LIST_COLUMNS], U16, name="offsets")
        nc.sync.dma_start(offsets[:], offs)
        own = [held.tile([P, TARGETS], F32, name=f"own{b}") for b in range(BLOCKS)]
        scores = [held.tile([P, NODES], F32, name=f"scores{b}") for b in range(BLOCKS)]
        values = [held.tile([P, NODES], F32, name=f"values{b}") for b in range(BLOCKS)]
        for b in (0, 1):
            rows = slice(b * P, (b + 1) * P)
            nc.sync.dma_start(own[b][:], t[rows, :])
            nc.sync.dma_start(scores[b][:], tab[1, rows, :])
        for b in range(BLOCKS):
            nc.sync.dma_start(values[b][:], tab[0, b * P:(b + 1) * P, :])

        zeros = held.tile([P, TARGETS], BF16, name="zeros")
        nc.vector.memset(zeros[:], 0.0)
        unread = sums.tile([P, TARGETS], F32, name="unread")
        for i in range(WARM_UPS):
            nc.tensor.matmul(unread[:], zeros[:, 0:P], zeros[:], start=True, stop=True)

        plus = held.tile([P, P], F32, name="plus")
        masks.make_identity(nc, plus[:])
        minus = held.tile([P, P], F32, name="minus")
        nc.gpsimd.tensor_scalar(minus[:], plus[:], -1.0, None, MULT)

        nothing = held.tile([P, 1], F32, name="nothing")
        nc.gpsimd.memset(nothing[:], 0.0)
        warmed = held.tile([P, 1], F32, name="warmed")
        nc.scalar.activation(warmed[:], nothing[:], SIGMOID)

        def entries(d, first, count):
            start = (d * TARGETS + first) // 16
            return offsets[:, start:start + count // 16]

        def tiles(kind):
            return [[held.tile([P, TARGETS], F32, name=f"{kind}{b}{d}") for d in range(NEIGHBOURS)] for b in range(BLOCKS)]

        a, bent, share, product = tiles("a"), tiles("bent"), tiles("share"), tiles("product")
        x = [held.tile([P, TARGETS], F32, name=f"x{b}") for b in range(BLOCKS)]
        halves = [slice(h * HALF, (h + 1) * HALF) for h in range(2)]

        def look_up_scores(b):
            for d in range(NEIGHBOURS):
                nc.vector.tensor_tensor(a[b][d][:], scores[b][:].indirect(entries(d, 0, TARGETS)), own[b][:], ADD)

        def make_shares(b, half, lead, scale):
            for d, sign in enumerate((1.0, -1.0)):
                nc.scalar.activation(share[b][d][:, half], lead, SIGMOID, scale=sign * scale)

        def weigh_on_tensor(b, h):
            half = halves[h]
            lead = sums.tile([P, HALF], F32, name=f"lead{b}{h}")
            for d, weights in enumerate((plus, minus)):
                nc.scalar.activation(bent[b][d][:, half], a[b][d][:, half], RELU, scale=1.0 / SLOPE - 1.0)
                nc.tensor.matmul(lead[:, 0:HALF], weights[:], a[b][d][:, half], start=d == 0, stop=False)
                nc.tensor.matmul(lead[:, 0:HALF], weights[:], bent[b][d][:, half], start=False, stop=d == 1)
            make_shares(b, half, lead[:, 0:HALF], SLOPE)

        def weigh_on_vector(b, h):
            half = halves[h]
            for d in range(NEIGHBOURS):
                nc.vector.scalar_tensor_tensor(bent[b][d][:, half], a[b][d][:, half], SLOPE, a[b][d][:, half], MULT, MAX)
            lead = held.tile([P, HALF], F32, name=f"lead{b}{h}")
            nc.vector.tensor_tensor(lead[:], bent[b][0][:, half], bent[b][1][:, half], SUB)
            make_shares(b, half, lead[:], 1.0)

        def look_up_values(b, h):
            half = halves[h]
            for d in range(NEIGHBOURS):
                picked = values[b][:].indirect(entries(d, h * HALF, HALF))
                nc.vector.tensor_tensor(product[b][d][:, half], picked, share[b][d][:, half], MULT)

        def add_on_tensor(b, h):
            half = halves[h]
            total = sums.tile([P, HALF], F32, name=f"total{b}{h}")
            for d in range(NEIGHBOURS):
                nc.tensor.matmul(total[:, 0:HALF], plus[:], product[b][d][:, half], start=d == 0, stop=d == 1)
            nc.scalar.copy(x[b][:, half], total[:, 0:HALF])

        def add_on_vector(b, h):
            half = halves[h]
            nc.vector.tensor_tensor(x[b][:, half], product[b][0][:, half], product[b][1][:, half], ADD)

        def store(b, h):
            nc.sync.dma_start(out[b * P:(b + 1) * P, halves[h]], x[b][:, halves[h]])

        look_up_scores(0)
        weigh_on_tensor(0, 0)
        weigh_on_tensor(0, 1)
        look_up_scores(1)
        weigh_on_vector(1, 0)
        weigh_on_tensor(1, 1)
        for b, h in ((0, 0), (1, 0), (0, 1)):
            look_up_values(b, h)
            add_on_tensor(b, h)
            store(b, h)
        look_up_values(1, 1)
        add_on_vector(1, 1)
        store(1, 1)
